import numpy as np
import ml_dtypes


def mxq(x, axis, fmt="e4m3"):
    dtype, down = {"e4m3": (ml_dtypes.float8_e4m3fn, 7), "e5m2": (ml_dtypes.float8_e5m2, 14)}[fmt]
    v = np.moveaxis(np.asarray(x, np.float32).astype(ml_dtypes.bfloat16).astype(np.float64), axis, -1)
    blocks = v.reshape(v.shape[:-1] + (-1, 32))
    amax = np.abs(blocks).max(-1, keepdims=True)
    byte = np.maximum(np.where(amax > 0, np.frexp(amax)[1] - 1 + 127, 0) - down, 1)
    scale = np.exp2(byte - 127.0)
    codes = (blocks / scale).astype(np.float32).astype(dtype).astype(np.float64)
    return np.moveaxis((codes * scale).reshape(v.shape), -1, axis)


WIDE = False


def mx_kscale(k):
    if not WIDE:
        return np.ones(k)
    levels = np.array([10, -10, 5, -5, 0])
    if k % 512:
        return np.exp2(np.random.permutation(np.resize(levels, k // 32))).repeat(32)
    a = np.empty((k // 512, 16))
    for p in range(k // 512):
        a[p, :8] = np.random.permutation(np.resize(levels, 8))
        for g in range(8):
            far = levels[np.abs(levels - a[p, g]) >= 10]
            a[p, g + 8] = far[np.random.randint(len(far))]
    return np.exp2(a.ravel()).repeat(32)


def f64(x):
    return np.asarray(x).astype(np.float64)


def striped8(idx):
    return np.asarray(idx).reshape(8, -1, 16).transpose(0, 2, 1).reshape(128, -1).astype(np.uint16)


def unstriped8(offs):
    return offs.reshape(8, 16, -1).transpose(0, 2, 1).reshape(8, -1).astype(np.int64)


def pick8(x, idx, run):
    r = np.arange(len(x))
    return x[r[:, None], idx[r % (8 * run) // run]]


E2M1 = np.array([0.0, 0.5, 1.0, 1.5, 2.0, 3.0, 4.0, 6.0, -0.0, -0.5, -1.0, -1.5, -2.0, -3.0, -4.0, -6.0])


def pack_weight(w, fmt):
    k, n = w.shape
    w = f64(np.asarray(w, np.float32).astype(ml_dtypes.bfloat16)).reshape(k // 32, 32, n)
    amax = np.abs(w).max(1)
    if fmt == "e4m3":
        byte = np.frexp(amax)[1] - 1 + 127 - 7
    else:
        mant, ex = np.frexp(amax / 6.0)
        byte = np.where(mant > 0.5, ex, ex - 1) + 127
    byte = np.clip(np.where(amax > 0, byte, 1), 1, 254)
    scaled = (w * np.exp2(127.0 - byte)[:, None, :]).reshape(k, n).astype(np.float32)
    by_word = np.ascontiguousarray(scaled.reshape(k // 512, 128, 4, n).transpose(0, 1, 3, 2))
    if fmt == "e4m3":
        words = by_word.astype(ml_dtypes.float8_e4m3fn).view(np.uint8)
    else:
        c = by_word.astype(ml_dtypes.float4_e2m1fn).view(np.uint8) & 0xF
        words = (c[..., 0::2] | (c[..., 1::2] << 4)).reshape(k // 512, 128, 2 * n)
    return np.ascontiguousarray(words), np.ascontiguousarray(byte.astype(np.uint8).reshape(k // 512, 16, n))


def unpack_weight(words, scales, fmt):
    g, _, n = scales.shape
    words = np.ascontiguousarray(words).reshape(g, 128, n, -1)
    if fmt == "e4m3":
        vals = words.view(ml_dtypes.float8_e4m3fn).astype(np.float64)
    else:
        nib = np.empty((g, 128, n, 4), np.uint8)
        nib[..., 0::2] = words & 0xF
        nib[..., 1::2] = words >> 4
        vals = E2M1[nib]
    vals = vals * np.repeat(np.exp2(scales.astype(np.float64) - 127.0), 8, axis=1)[..., None]
    return vals.transpose(0, 1, 3, 2).reshape(g * 512, n)


D, T, I, Q, G = 512, 1024, 512, 128, 64


def setup_inputs():
    n = np.random.standard_normal
    idx = np.stack([np.random.permutation(T)[:I] for _ in range(8)])
    idx2 = np.stack([np.random.permutation(T)[:I] for _ in range(8)])
    idx3 = np.stack([np.random.permutation(T)[:I] for _ in range(8)])
    fd = mx_kscale(D)
    keysp = pack_weight(n((D, T)) / fd[:, None], "e2m1")
    return {
        "query": (n((D, Q)) * 0.9 / np.sqrt(D) * fd[:, None]).astype(np.float32),
        "keys_words": keysp[0],
        "keys_scales": keysp[1],
        "lam": (np.random.uniform(0.7, 1.3, (Q, 1))).astype(np.float32),
        "old": (np.random.uniform(0.0, 2.0, (Q, T))).astype(np.float32),
        "fade": (np.random.uniform(0.3, 0.9, (Q, 1))).astype(np.float32),
        "offs": striped8(idx),
        "offs2": striped8(idx2),
        "offs3": striped8(idx3),
    }


def reference(query, keys_words, keys_scales, lam, old, fade, offs, offs2, offs3):
    idx = unstriped8(offs)
    idx2 = unstriped8(offs2)
    idx3 = unstriped8(offs3)
    keysu = unpack_weight(keys_words, keys_scales, "e2m1")
    queryq = mxq(f64(query), 0, "e4m3")
    a = queryq.T @ keysu
    s = pick8(a, idx, 16) * f64(lam) - np.abs(pick8(a, idx2, 16) - pick8(a, idx3, 16))
    p = np.exp(s)
    pg = p.reshape(Q, G, I // G).sum(axis=2)
    z0 = np.sum(pg, axis=1, keepdims=True)
    k0 = 1.0 / (z0 - pg)
    kr = np.repeat(k0, I // G, axis=1)
    w = p * kr
    ws = w * 64.0
    wf = np.zeros((Q, T))
    wf[np.arange(Q)[:, None], idx[np.arange(Q) % 128 // 16]] = ws
    y = f64(old) * f64(fade) + wf
    return y

@@ -1,0 +1,154 @@
+from contextlib import ExitStack
+
+import concourse.mybir as mybir
+
+D, T, I, Q, G = 512, 1024, 512, 128, 64
+FLOPS = 2 * D * Q * T
+
+F32 = mybir.dt.float32
+BF16 = mybir.dt.bfloat16
+I32 = mybir.dt.int32
+U32 = mybir.dt.uint32
+U16 = mybir.dt.uint16
+U8 = mybir.dt.uint8
+FP8X4 = mybir.dt.float8_e4m3fn_x4
+FP4X4 = mybir.dt.float4_e2m1fn_x4
+ALU = mybir.AluOpType
+ACT = mybir.ActivationFunctionType
+AXIS = mybir.AxisListType
+
+P = 128
+PACK = 4
+RUN = I // G
+HALF = I // 2
+HALF_G = G // 2
+HALF_COLS = HALF // 16
+N_MM = 256
+N_OUT = 256
+
+
+def tile_attend_betweentwo_outside_counts_heads_kernel(
+    tc, query, keys_words, keys_scales, lam, old, fade, offs, offs2, offs3, out
+):
+    nc = tc.nc
+    with ExitStack() as ctx:
+        lists = ctx.enter_context(tc.tile_pool(name="lists", bufs=1))
+        sb = ctx.enter_context(tc.tile_pool(name="sb", bufs=1))
+        ps = ctx.enter_context(tc.psum_pool(name="ps", bufs=1))
+
+        q_raw = sb.tile([P, PACK, Q], F32, name="q_raw")
+        k_words = sb.tile([P, 2 * T], U8, name="k_words", align_bytes=64)
+        k_scales = sb.tile([P, T], U8, name="k_scales", align_bytes=64)
+        idx1 = lists.tile([P, I // 16], U16, name="idx1")
+        idx2 = lists.tile([P, I // 16], U16, name="idx2")
+        idx3 = lists.tile([P, I // 16], U16, name="idx3")
+        lam_sb = sb.tile([P, 1], F32, name="lam_sb")
+        fade_sb = sb.tile([P, 1], F32, name="fade_sb")
+        old_sb = sb.tile([P, T], F32, name="old_sb")
+        placed = sb.tile([P, T], F32, name="placed")
+
+        nc.vector.memset(k_scales[:].bitcast(I32), 0)
+        nc.sync.dma_start(out=q_raw[:], in_=query.rearrange("(p j) w -> p j w", j=PACK))
+        for quad in range(4):
+            nc.scalar.dma_start(
+                out=k_scales[32 * quad : 32 * quad + 4, :].bitcast(I32),
+                in_=keys_scales[0, 4 * quad : 4 * quad + 4, :].bitcast(I32),
+            )
+        nc.sync.dma_start(out=k_words[:].bitcast(I32), in_=keys_words[0].bitcast(I32))
+        nc.sync.dma_start(idx2[:], offs2)
+        nc.sync.dma_start(idx3[:], offs3)
+        nc.sync.dma_start(idx1[:], offs)
+        nc.sync.dma_start(out=old_sb[:], in_=old)
+        nc.gpsimd.dma_start(out=lam_sb[:], in_=lam)
+        nc.gpsimd.dma_start(out=fade_sb[:], in_=fade)
+        nc.vector.memset(placed[:], 0.0)
+
+        q_bf = sb.tile([P, Q, PACK], BF16, name="q_bf", align_bytes=64)
+        q_codes = sb.tile([P, Q], U32, name="q_codes", align_bytes=64)
+        q_scales = sb.tile([P, Q], U8, name="q_scales", align_bytes=64)
+        nc.vector.tensor_copy(out=q_bf[:], in_=q_raw[:].rearrange("p j w -> p w j"))
+        nc.vector.quantize_mx(
+            out=q_codes[:].bitcast(FP8X4), scales=q_scales[:], in_=q_bf[:].rearrange("p w j -> p (w j)")
+        )
+
+        a = sb.tile([P, T], F32, name="a")
+        for n in range(T // N_MM):
+            cols = slice(n * N_MM, (n + 1) * N_MM)
+            bank = ps.tile([P, N_MM], F32, name=f"bank{n}")
+            nc.tensor.matmul_mx(
+                out=bank[:],
+                lhsT=q_codes[:].bitcast(FP8X4),
+                lhsT_scale=q_scales[:],
+                rhs=k_words[:, 2 * n * N_MM : 2 * (n + 1) * N_MM].bitcast(FP4X4),
+                rhs_scale=k_scales[:, cols],
+                start=True,
+                stop=True,
+            )
+            if n % 2 == 0:
+                nc.scalar.activation(out=a[:, cols], in_=bank[:], func=ACT.Copy)
+            else:
+                nc.vector.tensor_copy(out=a[:, cols], in_=bank[:])
+
+        def halves(name, width):
+            return [sb.tile([P, width], F32, name=f"{name}{h}") for h in range(2)]
+
+        def part(idx, h):
+            return idx[:, h * HALF_COLS : (h + 1) * HALF_COLS]
+
+        first, second, diff, dist, score, p, kr = (
+            halves(name, HALF) for name in ("first", "second", "diff", "dist", "score", "p", "kr")
+        )
+        pg, neg_den, neg_k = (halves(name, HALF_G) for name in ("pg", "neg_den", "neg_k"))
+        z = halves("z", 1)
+
+        nc.scalar.activation(out=second[0][:], in_=a[:].indirect(part(idx2, 0)), func=ACT.Copy)
+        nc.vector.tensor_copy(out=second[1][:], in_=a[:].indirect(part(idx2, 1)))
+        for h in range(2):
+            nc.vector.tensor_tensor(
+                out=diff[h][:], in0=a[:].indirect(part(idx3, h)), in1=second[h][:], op=ALU.subtract
+            )
+        for h in range(2):
+            nc.scalar.activation(out=first[h][:], in_=a[:].indirect(part(idx1, h)), func=ACT.Copy)
+            nc.scalar.activation(out=dist[h][:], in_=diff[h][:], func=ACT.Abs)
+            nc.vector.scalar_tensor_tensor(
+                out=score[h][:], in0=first[h][:], scalar=lam_sb[:], in1=dist[h][:], op0=ALU.mult, op1=ALU.subtract
+            )
+
+        def run_sums(h):
+            nc.vector.tensor_reduce(
+                out=pg[h][:], in_=p[h][:].rearrange("p (g r) -> p g r", r=RUN), axis=AXIS.X, op=ALU.add
+            )
+
+        def outside(h):
+            nc.vector.tensor_scalar(
+                out=neg_den[h][:], in0=pg[h][:], scalar1=z[0][:], scalar2=z[1][:], op0=ALU.subtract, op1=ALU.subtract
+            )
+
+        def invert(h):
+            nc.vector.reciprocal(out=neg_k[h][:], in_=neg_den[h][:])
+            nc.scalar.activation(
+                out=kr[h][:].rearrange("p (g r) -> p g r", r=RUN),
+                in_=neg_k[h][:].unsqueeze(2).to_broadcast([P, HALF_G, RUN]),
+                func=ACT.Copy,
+                scale=-64.0,
+            )
+
+        for h in range(2):
+            nc.scalar.activation(out=p[h][:], in_=score[h][:], func=ACT.Exp, accum_out=z[h][:])
+        run_sums(0)
+        outside(0)
+        run_sums(1)
+        invert(0)
+        outside(1)
+        invert(1)
+        for h in range(2):
+            nc.vector.tensor_tensor(out=placed[:].indirect(part(idx1, h)), in0=p[h][:], in1=kr[h][:], op=ALU.mult)
+
+        for n in range(T // N_OUT):
+            cols = slice(n * N_OUT, (n + 1) * N_OUT)
+            y = sb.tile([P, N_OUT], F32, name=f"y{n}")
+            nc.vector.scalar_tensor_tensor(
+                out=y[:], in0=old_sb[:, cols], scalar=fade_sb[:], in1=placed[:, cols], op0=ALU.mult, op1=ALU.add
+            )
+            queue = nc.sync if n % 2 == 0 else nc.scalar
+            queue.dma_start(out=out[:, cols], in_=y[:])

@@ -23,8 +23,9 @@ RUN = I // G
 HALF = I // 2
 HALF_G = G // 2
 HALF_COLS = HALF // 16
-N_MM = 256
-N_OUT = 256
+MM_WIDTHS = (256, 256, 256, 128, 128)
+OUT_WIDTHS = (128, 256, 256, 256, 128)
+LEAD = 128
 
 
 def tile_attend_betweentwo_outside_counts_heads_kernel(
@@ -36,7 +37,7 @@ def tile_attend_betweentwo_outside_counts_heads_kernel(
         sb = ctx.enter_context(tc.tile_pool(name="sb", bufs=1))
         ps = ctx.enter_context(tc.psum_pool(name="ps", bufs=1))
 
-        q_raw = sb.tile([P, PACK, Q], F32, name="q_raw")
+        q_raw = sb.tile([P, PACK, Q], F32, name="q_raw", tag="staged")
         k_words = sb.tile([P, 2 * T], U8, name="k_words", align_bytes=64)
         k_scales = sb.tile([P, T], U8, name="k_scales", align_bytes=64)
         idx1 = lists.tile([P, I // 16], U16, name="idx1")
@@ -44,10 +45,8 @@ def tile_attend_betweentwo_outside_counts_heads_kernel(
         idx3 = lists.tile([P, I // 16], U16, name="idx3")
         lam_sb = sb.tile([P, 1], F32, name="lam_sb")
         fade_sb = sb.tile([P, 1], F32, name="fade_sb")
-        old_sb = sb.tile([P, T], F32, name="old_sb")
         placed = sb.tile([P, T], F32, name="placed")
 
-        nc.vector.memset(k_scales[:].bitcast(I32), 0)
         nc.sync.dma_start(out=q_raw[:], in_=query.rearrange("(p j) w -> p j w", j=PACK))
         for quad in range(4):
             nc.scalar.dma_start(
@@ -58,28 +57,31 @@ def tile_attend_betweentwo_outside_counts_heads_kernel(
         nc.sync.dma_start(idx2[:], offs2)
         nc.sync.dma_start(idx3[:], offs3)
         nc.sync.dma_start(idx1[:], offs)
-        nc.sync.dma_start(out=old_sb[:], in_=old)
-        nc.gpsimd.dma_start(out=lam_sb[:], in_=lam)
-        nc.gpsimd.dma_start(out=fade_sb[:], in_=fade)
+        nc.sync.dma_start(out=lam_sb[:], in_=lam)
+        nc.sync.dma_start(out=fade_sb[:], in_=fade)
         nc.vector.memset(placed[:], 0.0)
 
         q_bf = sb.tile([P, Q, PACK], BF16, name="q_bf", align_bytes=64)
         q_codes = sb.tile([P, Q], U32, name="q_codes", align_bytes=64)
         q_scales = sb.tile([P, Q], U8, name="q_scales", align_bytes=64)
-        nc.vector.tensor_copy(out=q_bf[:], in_=q_raw[:].rearrange("p j w -> p w j"))
+        nc.vector.tensor_copy(
+            out=q_bf[:].rearrange("p (c i) j -> p c j i", i=4), in_=q_raw[:].rearrange("p j (c i) -> p c j i", i=4)
+        )
+        old_sb = sb.tile([P, T], F32, name="old_sb", tag="staged")
+        nc.sync.dma_start(out=old_sb[:], in_=old)
         nc.vector.quantize_mx(
             out=q_codes[:].bitcast(FP8X4), scales=q_scales[:], in_=q_bf[:].rearrange("p w j -> p (w j)")
         )
 
         a = sb.tile([P, T], F32, name="a")
-        for n in range(T // N_MM):
-            cols = slice(n * N_MM, (n + 1) * N_MM)
-            bank = ps.tile([P, N_MM], F32, name=f"bank{n}")
+        for n, width in enumerate(MM_WIDTHS):
+            cols = slice(sum(MM_WIDTHS[:n]), sum(MM_WIDTHS[: n + 1]))
+            bank = ps.tile([P, width], F32, name=f"bank{n}")
             nc.tensor.matmul_mx(
                 out=bank[:],
                 lhsT=q_codes[:].bitcast(FP8X4),
                 lhsT_scale=q_scales[:],
-                rhs=k_words[:, 2 * n * N_MM : 2 * (n + 1) * N_MM].bitcast(FP4X4),
+                rhs=k_words[:, 2 * cols.start : 2 * cols.stop].bitcast(FP4X4),
                 rhs_scale=k_scales[:, cols],
                 start=True,
                 stop=True,
@@ -95,14 +97,18 @@ def tile_attend_betweentwo_outside_counts_heads_kernel(
         def part(idx, h):
             return idx[:, h * HALF_COLS : (h + 1) * HALF_COLS]
 
-        first, second, diff, dist, score, p, kr = (
-            halves(name, HALF) for name in ("first", "second", "diff", "dist", "score", "p", "kr")
+        first, second, diff, dist, score = (
+            halves(name, HALF) for name in ("first", "second", "diff", "dist", "score")
         )
-        pg, neg_den, neg_k = (halves(name, HALF_G) for name in ("pg", "neg_den", "neg_k"))
         z = halves("z", 1)
+        p = sb.tile([P, I], F32, name="p")
+        kr = sb.tile([P, I], F32, name="kr")
+        pg = sb.tile([P, G], F32, name="pg")
+        neg_den = sb.tile([P, G], F32, name="neg_den")
+        neg_k = sb.tile([P, G], F32, name="neg_k")
 
-        nc.scalar.activation(out=second[0][:], in_=a[:].indirect(part(idx2, 0)), func=ACT.Copy)
-        nc.vector.tensor_copy(out=second[1][:], in_=a[:].indirect(part(idx2, 1)))
+        nc.vector.tensor_copy(out=second[0][:], in_=a[:].indirect(part(idx2, 0)))
+        nc.scalar.activation(out=second[1][:], in_=a[:].indirect(part(idx2, 1)), func=ACT.Copy)
         for h in range(2):
             nc.vector.tensor_tensor(
                 out=diff[h][:], in0=a[:].indirect(part(idx3, h)), in1=second[h][:], op=ALU.subtract
@@ -114,39 +120,52 @@ def tile_attend_betweentwo_outside_counts_heads_kernel(
                 out=score[h][:], in0=first[h][:], scalar=lam_sb[:], in1=dist[h][:], op0=ALU.mult, op1=ALU.subtract
             )
 
-        def run_sums(h):
+        def runs(lo, hi):
+            return slice(lo // RUN, hi // RUN)
+
+        def run_sums(lo, hi):
             nc.vector.tensor_reduce(
-                out=pg[h][:], in_=p[h][:].rearrange("p (g r) -> p g r", r=RUN), axis=AXIS.X, op=ALU.add
+                out=pg[:, runs(lo, hi)], in_=p[:, lo:hi].rearrange("p (g r) -> p g r", r=RUN), axis=AXIS.X, op=ALU.add
             )
 
-        def outside(h):
+        def outside(lo, hi):
             nc.vector.tensor_scalar(
-                out=neg_den[h][:], in0=pg[h][:], scalar1=z[0][:], scalar2=z[1][:], op0=ALU.subtract, op1=ALU.subtract
+                out=neg_den[:, runs(lo, hi)],
+                in0=pg[:, runs(lo, hi)],
+                scalar1=z[0][:],
+                scalar2=z[1][:],
+                op0=ALU.subtract,
+                op1=ALU.subtract,
             )
 
-        def invert(h):
-            nc.vector.reciprocal(out=neg_k[h][:], in_=neg_den[h][:])
+        def invert(lo, hi):
+            nc.vector.reciprocal(out=neg_k[:, runs(lo, hi)], in_=neg_den[:, runs(lo, hi)])
             nc.scalar.activation(
-                out=kr[h][:].rearrange("p (g r) -> p g r", r=RUN),
-                in_=neg_k[h][:].unsqueeze(2).to_broadcast([P, HALF_G, RUN]),
+                out=kr[:, lo:hi].rearrange("p (g r) -> p g r", r=RUN),
+                in_=neg_k[:, runs(lo, hi)].unsqueeze(2).to_broadcast([P, (hi - lo) // RUN, RUN]),
                 func=ACT.Copy,
                 scale=-64.0,
             )
 
         for h in range(2):
-            nc.scalar.activation(out=p[h][:], in_=score[h][:], func=ACT.Exp, accum_out=z[h][:])
-        run_sums(0)
-        outside(0)
-        run_sums(1)
-        invert(0)
-        outside(1)
-        invert(1)
-        for h in range(2):
-            nc.vector.tensor_tensor(out=placed[:].indirect(part(idx1, h)), in0=p[h][:], in1=kr[h][:], op=ALU.mult)
+            nc.scalar.activation(
+                out=p[:, h * HALF : (h + 1) * HALF], in_=score[h][:], func=ACT.Exp, accum_out=z[h][:]
+            )
+        run_sums(0, HALF)
+        outside(0, HALF)
+        run_sums(HALF, I)
+        invert(0, LEAD)
+        invert(LEAD, HALF)
+        outside(HALF, I)
+        invert(HALF, I)
+        for lo, hi in ((0, LEAD), (LEAD, I)):
+            nc.vector.tensor_tensor(
+                out=placed[:].indirect(idx1[:, lo // 16 : hi // 16]), in0=p[:, lo:hi], in1=kr[:, lo:hi], op=ALU.mult
+            )
 
-        for n in range(T // N_OUT):
-            cols = slice(n * N_OUT, (n + 1) * N_OUT)
-            y = sb.tile([P, N_OUT], F32, name=f"y{n}")
+        for n, width in enumerate(OUT_WIDTHS):
+            cols = slice(sum(OUT_WIDTHS[:n]), sum(OUT_WIDTHS[: n + 1]))
+            y = sb.tile([P, width], F32, name=f"y{n}")
             nc.vector.scalar_tensor_tensor(
                 out=y[:], in0=old_sb[:, cols], scalar=fade_sb[:], in1=placed[:, cols], op0=ALU.mult, op1=ALU.add
             )

@@ -19,13 +19,19 @@ AXIS = mybir.AxisListType
 
 P = 128
 PACK = 4
+QUADS = 4
+LINE = 4
+PER_COLUMN = 16
 RUN = I // G
+WEIGHT_SCALE = 64.0
 HALF = I // 2
-HALF_G = G // 2
-HALF_COLS = HALF // 16
-MM_WIDTHS = (256, 256, 256, 128, 128)
-OUT_WIDTHS = (128, 256, 256, 256, 128)
+PASS_WIDTHS = (256, 256, 256, 128, 128)
 LEAD = 128
+STORE_WIDTHS = (128, 256, 256, 256, 128)
+
+
+def pieces(widths):
+    return [slice(sum(widths[:n]), sum(widths[: n + 1])) for n in range(len(widths))]
 
 
 def tile_attend_betweentwo_outside_counts_heads_kernel(
@@ -38,22 +44,23 @@ def tile_attend_betweentwo_outside_counts_heads_kernel(
         ps = ctx.enter_context(tc.psum_pool(name="ps", bufs=1))
 
         q_raw = sb.tile([P, PACK, Q], F32, name="q_raw", tag="staged")
-        k_words = sb.tile([P, 2 * T], U8, name="k_words", align_bytes=64)
+        k_words = [sb.tile([P, T], U8, name=f"k_words{h}", align_bytes=64) for h in range(2)]
         k_scales = sb.tile([P, T], U8, name="k_scales", align_bytes=64)
-        idx1 = lists.tile([P, I // 16], U16, name="idx1")
-        idx2 = lists.tile([P, I // 16], U16, name="idx2")
-        idx3 = lists.tile([P, I // 16], U16, name="idx3")
+        idx1 = lists.tile([P, I // PER_COLUMN], U16, name="idx1")
+        idx2 = lists.tile([P, I // PER_COLUMN], U16, name="idx2")
+        idx3 = lists.tile([P, I // PER_COLUMN], U16, name="idx3")
         lam_sb = sb.tile([P, 1], F32, name="lam_sb")
         fade_sb = sb.tile([P, 1], F32, name="fade_sb")
         placed = sb.tile([P, T], F32, name="placed")
 
         nc.sync.dma_start(out=q_raw[:], in_=query.rearrange("(p j) w -> p j w", j=PACK))
-        for quad in range(4):
+        for h in range(2):
+            nc.sync.dma_start(out=k_words[h][:].bitcast(I32), in_=keys_words[0, :, h * T : (h + 1) * T].bitcast(I32))
+        for quad in range(QUADS):
             nc.scalar.dma_start(
                 out=k_scales[32 * quad : 32 * quad + 4, :].bitcast(I32),
                 in_=keys_scales[0, 4 * quad : 4 * quad + 4, :].bitcast(I32),
             )
-        nc.sync.dma_start(out=k_words[:].bitcast(I32), in_=keys_words[0].bitcast(I32))
         nc.sync.dma_start(idx2[:], offs2)
         nc.sync.dma_start(idx3[:], offs3)
         nc.sync.dma_start(idx1[:], offs)
@@ -64,24 +71,30 @@ def tile_attend_betweentwo_outside_counts_heads_kernel(
         q_bf = sb.tile([P, Q, PACK], BF16, name="q_bf", align_bytes=64)
         q_codes = sb.tile([P, Q], U32, name="q_codes", align_bytes=64)
         q_scales = sb.tile([P, Q], U8, name="q_scales", align_bytes=64)
-        nc.vector.tensor_copy(
-            out=q_bf[:].rearrange("p (c i) j -> p c j i", i=4), in_=q_raw[:].rearrange("p j (c i) -> p c j i", i=4)
-        )
+        row_halves = pieces((Q // 2, Q // 2))
+        for rows in row_halves:
+            nc.vector.tensor_copy(
+                out=q_bf[:, rows, :].rearrange("p (c i) j -> p c j i", i=LINE),
+                in_=q_raw[:, :, rows].rearrange("p j (c i) -> p c j i", i=LINE),
+            )
         old_sb = sb.tile([P, T], F32, name="old_sb", tag="staged")
         nc.sync.dma_start(out=old_sb[:], in_=old)
-        nc.vector.quantize_mx(
-            out=q_codes[:].bitcast(FP8X4), scales=q_scales[:], in_=q_bf[:].rearrange("p w j -> p (w j)")
-        )
+        for rows in row_halves:
+            nc.vector.quantize_mx(
+                out=q_codes[:, rows].bitcast(FP8X4),
+                scales=q_scales[:, rows],
+                in_=q_bf[:, rows, :].rearrange("p w j -> p (w j)"),
+            )
 
         a = sb.tile([P, T], F32, name="a")
-        for n, width in enumerate(MM_WIDTHS):
-            cols = slice(sum(MM_WIDTHS[:n]), sum(MM_WIDTHS[: n + 1]))
-            bank = ps.tile([P, width], F32, name=f"bank{n}")
+        for n, cols in enumerate(pieces(PASS_WIDTHS)):
+            bank = ps.tile([P, cols.stop - cols.start], F32, name=f"bank{n}")
+            h, start = divmod(2 * cols.start, T)
             nc.tensor.matmul_mx(
                 out=bank[:],
                 lhsT=q_codes[:].bitcast(FP8X4),
                 lhsT_scale=q_scales[:],
-                rhs=k_words[:, 2 * cols.start : 2 * cols.stop].bitcast(FP4X4),
+                rhs=k_words[h][:, start : start + 2 * (cols.stop - cols.start)].bitcast(FP4X4),
                 rhs_scale=k_scales[:, cols],
                 start=True,
                 stop=True,
@@ -94,31 +107,32 @@ def tile_attend_betweentwo_outside_counts_heads_kernel(
         def halves(name, width):
             return [sb.tile([P, width], F32, name=f"{name}{h}") for h in range(2)]
 
-        def part(idx, h):
-            return idx[:, h * HALF_COLS : (h + 1) * HALF_COLS]
+        def entries(idx, lo, hi):
+            return idx[:, lo // PER_COLUMN : hi // PER_COLUMN]
+
+        def look_up(idx, h):
+            return a[:].indirect(entries(idx, h * HALF, (h + 1) * HALF))
 
         first, second, diff, dist, score = (
             halves(name, HALF) for name in ("first", "second", "diff", "dist", "score")
         )
-        z = halves("z", 1)
-        p = sb.tile([P, I], F32, name="p")
-        kr = sb.tile([P, I], F32, name="kr")
-        pg = sb.tile([P, G], F32, name="pg")
-        neg_den = sb.tile([P, G], F32, name="neg_den")
-        neg_k = sb.tile([P, G], F32, name="neg_k")
-
-        nc.vector.tensor_copy(out=second[0][:], in_=a[:].indirect(part(idx2, 0)))
-        nc.scalar.activation(out=second[1][:], in_=a[:].indirect(part(idx2, 1)), func=ACT.Copy)
+        nc.vector.tensor_copy(out=second[0][:], in_=look_up(idx2, 0))
+        nc.scalar.activation(out=second[1][:], in_=look_up(idx2, 1), func=ACT.Copy)
         for h in range(2):
-            nc.vector.tensor_tensor(
-                out=diff[h][:], in0=a[:].indirect(part(idx3, h)), in1=second[h][:], op=ALU.subtract
-            )
+            nc.vector.tensor_tensor(out=diff[h][:], in0=look_up(idx3, h), in1=second[h][:], op=ALU.subtract)
         for h in range(2):
-            nc.scalar.activation(out=first[h][:], in_=a[:].indirect(part(idx1, h)), func=ACT.Copy)
+            nc.scalar.activation(out=first[h][:], in_=look_up(idx1, h), func=ACT.Copy)
             nc.scalar.activation(out=dist[h][:], in_=diff[h][:], func=ACT.Abs)
             nc.vector.scalar_tensor_tensor(
                 out=score[h][:], in0=first[h][:], scalar=lam_sb[:], in1=dist[h][:], op0=ALU.mult, op1=ALU.subtract
             )
+
+        z = halves("z", 1)
+        p = sb.tile([P, I], F32, name="p")
+        pg = sb.tile([P, G], F32, name="pg")
+        neg_outside = sb.tile([P, G], F32, name="neg_outside")
+        neg_k0 = sb.tile([P, G], F32, name="neg_k0")
+        factor = sb.tile([P, I], F32, name="factor")
 
         def runs(lo, hi):
             return slice(lo // RUN, hi // RUN)
@@ -128,9 +142,9 @@ def tile_attend_betweentwo_outside_counts_heads_kernel(
                 out=pg[:, runs(lo, hi)], in_=p[:, lo:hi].rearrange("p (g r) -> p g r", r=RUN), axis=AXIS.X, op=ALU.add
             )
 
-        def outside(lo, hi):
+        def outside_sums(lo, hi):
             nc.vector.tensor_scalar(
-                out=neg_den[:, runs(lo, hi)],
+                out=neg_outside[:, runs(lo, hi)],
                 in0=pg[:, runs(lo, hi)],
                 scalar1=z[0][:],
                 scalar2=z[1][:],
@@ -138,13 +152,13 @@ def tile_attend_betweentwo_outside_counts_heads_kernel(
                 op1=ALU.subtract,
             )
 
-        def invert(lo, hi):
-            nc.vector.reciprocal(out=neg_k[:, runs(lo, hi)], in_=neg_den[:, runs(lo, hi)])
+        def factors(lo, hi):
+            nc.vector.reciprocal(out=neg_k0[:, runs(lo, hi)], in_=neg_outside[:, runs(lo, hi)])
             nc.scalar.activation(
-                out=kr[:, lo:hi].rearrange("p (g r) -> p g r", r=RUN),
-                in_=neg_k[:, runs(lo, hi)].unsqueeze(2).to_broadcast([P, (hi - lo) // RUN, RUN]),
+                out=factor[:, lo:hi].rearrange("p (g r) -> p g r", r=RUN),
+                in_=neg_k0[:, runs(lo, hi)].unsqueeze(2).to_broadcast([P, (hi - lo) // RUN, RUN]),
                 func=ACT.Copy,
-                scale=-64.0,
+                scale=-WEIGHT_SCALE,
             )
 
         for h in range(2):
@@ -152,20 +166,20 @@ def tile_attend_betweentwo_outside_counts_heads_kernel(
                 out=p[:, h * HALF : (h + 1) * HALF], in_=score[h][:], func=ACT.Exp, accum_out=z[h][:]
             )
         run_sums(0, HALF)
-        outside(0, HALF)
+        outside_sums(0, HALF)
         run_sums(HALF, I)
-        invert(0, LEAD)
-        invert(LEAD, HALF)
-        outside(HALF, I)
-        invert(HALF, I)
+        factors(0, LEAD)
+        factors(LEAD, HALF)
+        outside_sums(HALF, I)
+        factors(HALF, I)
+
         for lo, hi in ((0, LEAD), (LEAD, I)):
             nc.vector.tensor_tensor(
-                out=placed[:].indirect(idx1[:, lo // 16 : hi // 16]), in0=p[:, lo:hi], in1=kr[:, lo:hi], op=ALU.mult
+                out=placed[:].indirect(entries(idx1, lo, hi)), in0=p[:, lo:hi], in1=factor[:, lo:hi], op=ALU.mult
             )
 
-        for n, width in enumerate(OUT_WIDTHS):
-            cols = slice(sum(OUT_WIDTHS[:n]), sum(OUT_WIDTHS[: n + 1]))
-            y = sb.tile([P, width], F32, name=f"y{n}")
+        for n, cols in enumerate(pieces(STORE_WIDTHS)):
+            y = sb.tile([P, cols.stop - cols.start], F32, name=f"y{n}")
             nc.vector.scalar_tensor_tensor(
                 out=y[:], in0=old_sb[:, cols], scalar=fade_sb[:], in1=placed[:, cols], op0=ALU.mult, op1=ALU.add
             )

from contextlib import ExitStack

import concourse.mybir as mybir

D, T, I, Q, G = 512, 1024, 512, 128, 64
FLOPS = 2 * D * Q * T

F32 = mybir.dt.float32
BF16 = mybir.dt.bfloat16
I32 = mybir.dt.int32
U32 = mybir.dt.uint32
U16 = mybir.dt.uint16
U8 = mybir.dt.uint8
FP8X4 = mybir.dt.float8_e4m3fn_x4
FP4X4 = mybir.dt.float4_e2m1fn_x4
ALU = mybir.AluOpType
ACT = mybir.ActivationFunctionType
AXIS = mybir.AxisListType

P = 128
PACK = 4
QUADS = 4
LINE = 4
PER_COLUMN = 16
RUN = I // G
WEIGHT_SCALE = 64.0
HALF = I // 2
PASS_WIDTHS = (256, 256, 256, 128, 128)
LEAD = 128
STORE_WIDTHS = (128, 256, 256, 256, 128)


def pieces(widths):
    return [slice(sum(widths[:n]), sum(widths[: n + 1])) for n in range(len(widths))]


def tile_attend_betweentwo_outside_counts_heads_kernel(
    tc, query, keys_words, keys_scales, lam, old, fade, offs, offs2, offs3, out
):
    nc = tc.nc
    with ExitStack() as ctx:
        lists = ctx.enter_context(tc.tile_pool(name="lists", bufs=1))
        sb = ctx.enter_context(tc.tile_pool(name="sb", bufs=1))
        ps = ctx.enter_context(tc.psum_pool(name="ps", bufs=1))

        q_raw = sb.tile([P, PACK, Q], F32, name="q_raw", tag="staged")
        k_words = [sb.tile([P, T], U8, name=f"k_words{h}", align_bytes=64) for h in range(2)]
        k_scales = sb.tile([P, T], U8, name="k_scales", align_bytes=64)
        idx1 = lists.tile([P, I // PER_COLUMN], U16, name="idx1")
        idx2 = lists.tile([P, I // PER_COLUMN], U16, name="idx2")
        idx3 = lists.tile([P, I // PER_COLUMN], U16, name="idx3")
        lam_sb = sb.tile([P, 1], F32, name="lam_sb")
        fade_sb = sb.tile([P, 1], F32, name="fade_sb")
        placed = sb.tile([P, T], F32, name="placed")

        nc.sync.dma_start(out=q_raw[:], in_=query.rearrange("(p j) w -> p j w", j=PACK))
        for h in range(2):
            nc.sync.dma_start(out=k_words[h][:].bitcast(I32), in_=keys_words[0, :, h * T : (h + 1) * T].bitcast(I32))
        for quad in range(QUADS):
            nc.scalar.dma_start(
                out=k_scales[32 * quad : 32 * quad + 4, :].bitcast(I32),
                in_=keys_scales[0, 4 * quad : 4 * quad + 4, :].bitcast(I32),
            )
        nc.sync.dma_start(idx2[:], offs2)
        nc.sync.dma_start(idx3[:], offs3)
        nc.sync.dma_start(idx1[:], offs)
        nc.sync.dma_start(out=lam_sb[:], in_=lam)
        nc.sync.dma_start(out=fade_sb[:], in_=fade)
        nc.vector.memset(placed[:], 0.0)

        q_bf = sb.tile([P, Q, PACK], BF16, name="q_bf", align_bytes=64)
        q_codes = sb.tile([P, Q], U32, name="q_codes", align_bytes=64)
        q_scales = sb.tile([P, Q], U8, name="q_scales", align_bytes=64)
        row_halves = pieces((Q // 2, Q // 2))
        for rows in row_halves:
            nc.vector.tensor_copy(
                out=q_bf[:, rows, :].rearrange("p (c i) j -> p c j i", i=LINE),
                in_=q_raw[:, :, rows].rearrange("p j (c i) -> p c j i", i=LINE),
            )
        old_sb = sb.tile([P, T], F32, name="old_sb", tag="staged")
        nc.sync.dma_start(out=old_sb[:], in_=old)
        for rows in row_halves:
            nc.vector.quantize_mx(
                out=q_codes[:, rows].bitcast(FP8X4),
                scales=q_scales[:, rows],
                in_=q_bf[:, rows, :].rearrange("p w j -> p (w j)"),
            )

        a = sb.tile([P, T], F32, name="a")
        for n, cols in enumerate(pieces(PASS_WIDTHS)):
            bank = ps.tile([P, cols.stop - cols.start], F32, name=f"bank{n}")
            h, start = divmod(2 * cols.start, T)
            nc.tensor.matmul_mx(
                out=bank[:],
                lhsT=q_codes[:].bitcast(FP8X4),
                lhsT_scale=q_scales[:],
                rhs=k_words[h][:, start : start + 2 * (cols.stop - cols.start)].bitcast(FP4X4),
                rhs_scale=k_scales[:, cols],
                start=True,
                stop=True,
            )
            if n % 2 == 0:
                nc.scalar.activation(out=a[:, cols], in_=bank[:], func=ACT.Copy)
            else:
                nc.vector.tensor_copy(out=a[:, cols], in_=bank[:])

        def halves(name, width):
            return [sb.tile([P, width], F32, name=f"{name}{h}") for h in range(2)]

        def entries(idx, lo, hi):
            return idx[:, lo // PER_COLUMN : hi // PER_COLUMN]

        def look_up(idx, h):
            return a[:].indirect(entries(idx, h * HALF, (h + 1) * HALF))

        first, second, diff, dist, score = (
            halves(name, HALF) for name in ("first", "second", "diff", "dist", "score")
        )
        nc.vector.tensor_copy(out=second[0][:], in_=look_up(idx2, 0))
        nc.scalar.activation(out=second[1][:], in_=look_up(idx2, 1), func=ACT.Copy)
        for h in range(2):
            nc.vector.tensor_tensor(out=diff[h][:], in0=look_up(idx3, h), in1=second[h][:], op=ALU.subtract)
        for h in range(2):
            nc.scalar.activation(out=first[h][:], in_=look_up(idx1, h), func=ACT.Copy)
            nc.scalar.activation(out=dist[h][:], in_=diff[h][:], func=ACT.Abs)
            nc.vector.scalar_tensor_tensor(
                out=score[h][:], in0=first[h][:], scalar=lam_sb[:], in1=dist[h][:], op0=ALU.mult, op1=ALU.subtract
            )

        z = halves("z", 1)
        p = sb.tile([P, I], F32, name="p")
        pg = sb.tile([P, G], F32, name="pg")
        neg_outside = sb.tile([P, G], F32, name="neg_outside")
        neg_k0 = sb.tile([P, G], F32, name="neg_k0")
        factor = sb.tile([P, I], F32, name="factor")

        def runs(lo, hi):
            return slice(lo // RUN, hi // RUN)

        def run_sums(lo, hi):
            nc.vector.tensor_reduce(
                out=pg[:, runs(lo, hi)], in_=p[:, lo:hi].rearrange("p (g r) -> p g r", r=RUN), axis=AXIS.X, op=ALU.add
            )

        def outside_sums(lo, hi):
            nc.vector.tensor_scalar(
                out=neg_outside[:, runs(lo, hi)],
                in0=pg[:, runs(lo, hi)],
                scalar1=z[0][:],
                scalar2=z[1][:],
                op0=ALU.subtract,
                op1=ALU.subtract,
            )

        def factors(lo, hi):
            nc.vector.reciprocal(out=neg_k0[:, runs(lo, hi)], in_=neg_outside[:, runs(lo, hi)])
            nc.scalar.activation(
                out=factor[:, lo:hi].rearrange("p (g r) -> p g r", r=RUN),
                in_=neg_k0[:, runs(lo, hi)].unsqueeze(2).to_broadcast([P, (hi - lo) // RUN, RUN]),
                func=ACT.Copy,
                scale=-WEIGHT_SCALE,
            )

        for h in range(2):
            nc.scalar.activation(
                out=p[:, h * HALF : (h + 1) * HALF], in_=score[h][:], func=ACT.Exp, accum_out=z[h][:]
            )
        run_sums(0, HALF)
        outside_sums(0, HALF)
        run_sums(HALF, I)
        factors(0, LEAD)
        factors(LEAD, HALF)
        outside_sums(HALF, I)
        factors(HALF, I)

        for lo, hi in ((0, LEAD), (LEAD, I)):
            nc.vector.tensor_tensor(
                out=placed[:].indirect(entries(idx1, lo, hi)), in0=p[:, lo:hi], in1=factor[:, lo:hi], op=ALU.mult
            )

        for n, cols in enumerate(pieces(STORE_WIDTHS)):
            y = sb.tile([P, cols.stop - cols.start], F32, name=f"y{n}")
            nc.vector.scalar_tensor_tensor(
                out=y[:], in0=old_sb[:, cols], scalar=fade_sb[:], in1=placed[:, cols], op0=ALU.mult, op1=ALU.add
            )
            queue = nc.sync if n % 2 == 0 else nc.scalar
            queue.dma_start(out=out[:, cols], in_=y[:])
